import numpy as np
import ml_dtypes


def mxq(x, axis, fmt="e4m3"):
    dtype, down = {"e4m3": (ml_dtypes.float8_e4m3fn, 7), "e5m2": (ml_dtypes.float8_e5m2, 14)}[fmt]
    v = np.moveaxis(np.asarray(x, np.float32).astype(ml_dtypes.bfloat16).astype(np.float64), axis, -1)
    blocks = v.reshape(v.shape[:-1] + (-1, 32))
    amax = np.abs(blocks).max(-1, keepdims=True)
    byte = np.maximum(np.where(amax > 0, np.frexp(amax)[1] - 1 + 127, 0) - down, 1)
    scale = np.exp2(byte - 127.0)
    codes = (blocks / scale).astype(np.float32).astype(dtype).astype(np.float64)
    return np.moveaxis((codes * scale).reshape(v.shape), -1, axis)


WIDE = False


def mx_kscale(k):
    if not WIDE:
        return np.ones(k)
    levels = np.array([30, -30])
    if k % 512:
        return np.exp2(np.random.permutation(np.resize(levels, k // 32))).repeat(32)
    a = np.empty((k // 512, 16))
    for p in range(k // 512):
        a[p, :8] = np.random.permutation(np.resize(levels, 8))
        for g in range(8):
            far = levels[np.abs(levels - a[p, g]) >= 10]
            a[p, g + 8] = far[np.random.randint(len(far))]
    return np.exp2(a.ravel()).repeat(32)


def f64(x):
    return np.asarray(x).astype(np.float64)


E2M1 = np.array([0.0, 0.5, 1.0, 1.5, 2.0, 3.0, 4.0, 6.0, -0.0, -0.5, -1.0, -1.5, -2.0, -3.0, -4.0, -6.0])


def pack_weight(w, fmt):
    k, n = w.shape
    w = f64(np.asarray(w, np.float32).astype(ml_dtypes.bfloat16)).reshape(k // 32, 32, n)
    amax = np.abs(w).max(1)
    if fmt == "e4m3":
        byte = np.frexp(amax)[1] - 1 + 127 - 7
    else:
        mant, ex = np.frexp(amax / 6.0)
        byte = np.where(mant > 0.5, ex, ex - 1) + 127
    byte = np.clip(np.where(amax > 0, byte, 1), 1, 254)
    scaled = (w * np.exp2(127.0 - byte)[:, None, :]).reshape(k, n).astype(np.float32)
    by_word = np.ascontiguousarray(scaled.reshape(k // 512, 128, 4, n).transpose(0, 1, 3, 2))
    if fmt == "e4m3":
        words = by_word.astype(ml_dtypes.float8_e4m3fn).view(np.uint8)
    else:
        c = by_word.astype(ml_dtypes.float4_e2m1fn).view(np.uint8) & 0xF
        words = (c[..., 0::2] | (c[..., 1::2] << 4)).reshape(k // 512, 128, 2 * n)
    return np.ascontiguousarray(words), np.ascontiguousarray(byte.astype(np.uint8).reshape(k // 512, 16, n))


def unpack_weight(words, scales, fmt):
    g, _, n = scales.shape
    words = np.ascontiguousarray(words).reshape(g, 128, n, -1)
    if fmt == "e4m3":
        vals = words.view(ml_dtypes.float8_e4m3fn).astype(np.float64)
    else:
        nib = np.empty((g, 128, n, 4), np.uint8)
        nib[..., 0::2] = words & 0xF
        nib[..., 1::2] = words >> 4
        vals = E2M1[nib]
    vals = vals * np.repeat(np.exp2(scales.astype(np.float64) - 127.0), 8, axis=1)[..., None]
    return vals.transpose(0, 1, 3, 2).reshape(g * 512, n)


O, K, M, T = 512, 1536, 1024, 512


def setup_inputs():
    n = np.random.standard_normal
    s = mx_kscale(K)[:, None]
    dy = np.exp(0.5 * n((1, T))) * n((K, T))
    w = n((K, M)) / np.sqrt(K) / s
    p_w8 = pack_weight(w[:O], "e4m3")
    p_w4 = pack_weight(w[O:], "e2m1")
    return {
        "dy": (dy * s).astype(np.float32),
        "w8_words": p_w8[0],
        "w8_scales": p_w8[1],
        "w4_words": p_w4[0],
        "w4_scales": p_w4[1],
    }


def reference(dy, w8_words, w8_scales, w4_words, w4_scales):
    dy_ = mxq(f64(dy), 0, "e5m2")
    w8_ = unpack_weight(w8_words, w8_scales, "e4m3")
    w4_ = unpack_weight(w4_words, w4_scales, "e2m1")
    y = w8_.T @ dy_[:O] + w4_.T @ dy_[O:]
    return y

@@ -1,0 +1,136 @@
+from contextlib import ExitStack
+
+import concourse.mybir as mybir
+
+F32 = mybir.dt.float32
+BF16 = mybir.dt.bfloat16
+I32 = mybir.dt.int32
+U32 = mybir.dt.uint32
+U8 = mybir.dt.uint8
+E4M3X4 = mybir.dt.float8_e4m3fn_x4
+E5M2X4 = mybir.dt.float8_e5m2_x4
+E2M1X4 = mybir.dt.float4_e2m1fn_x4
+
+P = 128
+PACK = 4
+K, D, T = 1536, 1024, 512
+D_TILES = D // P
+CHUNKS = {1: [256,256], 2: [256,256], 0: [256,256]}
+V_SHARE = {128: 88, 256: 176, 384: 264, 512: 352}
+
+FLOPS = 2 * K * D * T
+BYTES = K * T * 4 + 512 * D + 1024 * D // 2 + 48 * D + D * T * 4
+
+
+def tile_mix_dyq_fm_none_kernel(tc, dy, w8_words, w8_scales, w4_words, w4_scales, out):
+    nc = tc.nc
+    with ExitStack() as ctx:
+        keep = ctx.enter_context(tc.tile_pool(name="keep", bufs=1))
+        psum = ctx.enter_context(tc.psum_pool(name="psum", bufs=1))
+        ctx.enter_context(tc.manual_schedule())
+
+        raw = []
+        grouped = []
+        codes = []
+        scales = []
+        spans = {}
+        for g in range(3):
+            edges = [sum(CHUNKS[g][:i]) for i in range(len(CHUNKS[g]) + 1)]
+            spans[g] = list(zip(edges[:-1], edges[1:]))
+            raw.append([keep.tile([P, PACK, b - a], F32, name="raw%d_%d" % (g, a), align_bytes=64) for a, b in spans[g]])
+            grouped.append([keep.tile([P, b - a, PACK], BF16, name="grouped%d_%d" % (g, a), align_bytes=64) for a, b in spans[g]])
+            codes.append(keep.tile([P, T], U32, name="codes%d" % g, align_bytes=64))
+            scales.append(keep.tile([P, T], U8, name="scales%d" % g, align_bytes=64))
+        w8 = keep.tile([P, D], U32, name="w8", align_bytes=64)
+        w4 = keep.tile([P, 2, 2 * D], U8, name="w4", align_bytes=64)
+        ws = keep.tile([P, 3, D], U8, name="ws", align_bytes=64)
+        warm = keep.tile([P, 8], F32, name="warm", align_bytes=64)
+        acc = [psum.tile([P, T], F32, name="acc%d" % m) for m in range(D_TILES)]
+        res = [keep.tile([P, T], F32, name="res%d" % m, align_bytes=64) for m in range(D_TILES)]
+
+        def load_dy(g, i):
+            a, b = spans[g][i]
+            rows = dy[512 * g : 512 * (g + 1), :].rearrange("(p j) t -> p j t", j=PACK)
+            nc.sync.dma_start(out=raw[g][i][:], in_=rows[:, :, a:b])
+
+        def load_w4(a):
+            nc.sync.dma_start(out=w4[:, a, :].bitcast(I32), in_=w4_words[a].bitcast(I32))
+
+        def load_ws4():
+            for r in range(4):
+                nc.sync.dma_start(
+                    out=ws[r:P:32, 1:3, :].bitcast(I32),
+                    in_=w4_scales[:, r:16:4, :].rearrange("a q d -> q a d").bitcast(I32),
+                )
+
+        def load_ws8():
+            for r in range(4):
+                nc.sync.dma_start(out=ws[r:P:32, 0, :].bitcast(I32), in_=w8_scales[0, r:16:4, :].bitcast(I32))
+
+        def load_w8(c, n):
+            cols = slice(c * D // n, (c + 1) * D // n)
+            nc.sync.dma_start(out=w8[:, cols].bitcast(I32), in_=w8_words[0].rearrange("p d t -> p (d t)").bitcast(I32)[:, cols])
+
+        nc.vector.memset(ws[:].rearrange("p g d -> p (g d)").bitcast(I32), 0)
+        nc.vector.memset(warm[:], 0.0)
+        nc.scalar.copy(warm[:, 4:5], warm[:, 0:1])
+
+        load_dy(1, 0)
+        load_dy(1, 1)
+        load_w4(0)
+        load_ws4()
+        load_w4(1)
+        load_dy(2, 0)
+        load_dy(2, 1)
+        load_dy(0, 0)
+        load_dy(0, 1)
+        load_ws8()
+        load_w8(0, 2)
+        load_w8(1, 2)
+
+        def interleave(g, i):
+            dst = grouped[g][i]
+            src = raw[g][i][:].rearrange("p j t -> p t j")
+            n = dst.shape[1]
+            v = V_SHARE[n]
+            nc.vector.tensor_copy(out=dst[:, 0:v, :], in_=src[:, 0:v, :])
+            nc.scalar.copy(dst[:, v:n, :], src[:, v:n, :])
+
+        def quantize(g, i):
+            a, b = spans[g][i]
+            nc.vector.quantize_mx(
+                out=codes[g][:, a:b].bitcast(E5M2X4),
+                scales=scales[g][:, a:b],
+                in_=grouped[g][i][:].rearrange("p t j -> p (t j)"),
+            )
+
+        def multiply(g, m, start, stop):
+            cols = slice(m * P, (m + 1) * P)
+            if g == 0:
+                lhsT = w8[:, cols].bitcast(E4M3X4)
+            else:
+                lhsT = w4[:, g - 1, 2 * m * P : 2 * (m + 1) * P].bitcast(E2M1X4)
+            nc.tensor.matmul_mx(
+                out=acc[m][:],
+                lhsT=lhsT,
+                lhsT_scale=ws[:, g, cols],
+                rhs=codes[g][:].bitcast(E5M2X4),
+                rhs_scale=scales[g][:],
+                start=start,
+                stop=stop,
+            )
+
+        for g in (1, 2, 0):
+            for i in range(len(spans[g])):
+                interleave(g, i)
+                quantize(g, i)
+            if g != 0:
+                for m in range(D_TILES):
+                    multiply(g, m, g == 1, False)
+        for m in range(D_TILES):
+            multiply(0, m, False, True)
+            if m % 2 == 0:
+                nc.vector.tensor_copy(out=res[m][:], in_=acc[m][:])
+            else:
+                nc.scalar.copy(res[m][:], acc[m][:])
+            nc.sync.dma_start(out=out[m * P : (m + 1) * P, :], in_=res[m][:])

@@ -15,8 +15,8 @@ P = 128
 PACK = 4
 K, D, T = 1536, 1024, 512
 D_TILES = D // P
-CHUNKS = {1: [256,256], 2: [256,256], 0: [256,256]}
-V_SHARE = {128: 88, 256: 176, 384: 264, 512: 352}
+HALF = T // 2
+V_COLS = 168
 
 FLOPS = 2 * K * D * T
 BYTES = K * T * 4 + 512 * D + 1024 * D // 2 + 48 * D + D * T * 4
@@ -33,12 +33,9 @@ def tile_mix_dyq_fm_none_kernel(tc, dy, w8_words, w8_scales, w4_words, w4_scales
         grouped = []
         codes = []
         scales = []
-        spans = {}
         for g in range(3):
-            edges = [sum(CHUNKS[g][:i]) for i in range(len(CHUNKS[g]) + 1)]
-            spans[g] = list(zip(edges[:-1], edges[1:]))
-            raw.append([keep.tile([P, PACK, b - a], F32, name="raw%d_%d" % (g, a), align_bytes=64) for a, b in spans[g]])
-            grouped.append([keep.tile([P, b - a, PACK], BF16, name="grouped%d_%d" % (g, a), align_bytes=64) for a, b in spans[g]])
+            raw.append(keep.tile([P, PACK, T], F32, name="raw%d" % g, align_bytes=64))
+            grouped.append([keep.tile([P, HALF, PACK], BF16, name="grouped%d%d" % (g, h), align_bytes=64) for h in range(2)])
             codes.append(keep.tile([P, T], U32, name="codes%d" % g, align_bytes=64))
             scales.append(keep.tile([P, T], U8, name="scales%d" % g, align_bytes=64))
         w8 = keep.tile([P, D], U32, name="w8", align_bytes=64)
@@ -48,60 +45,47 @@ def tile_mix_dyq_fm_none_kernel(tc, dy, w8_words, w8_scales, w4_words, w4_scales
         acc = [psum.tile([P, T], F32, name="acc%d" % m) for m in range(D_TILES)]
         res = [keep.tile([P, T], F32, name="res%d" % m, align_bytes=64) for m in range(D_TILES)]
 
-        def load_dy(g, i):
-            a, b = spans[g][i]
+        def load_dy(g, c0, c1):
             rows = dy[512 * g : 512 * (g + 1), :].rearrange("(p j) t -> p j t", j=PACK)
-            nc.sync.dma_start(out=raw[g][i][:], in_=rows[:, :, a:b])
-
-        def load_w4(a):
-            nc.sync.dma_start(out=w4[:, a, :].bitcast(I32), in_=w4_words[a].bitcast(I32))
-
-        def load_ws4():
-            for r in range(4):
-                nc.sync.dma_start(
-                    out=ws[r:P:32, 1:3, :].bitcast(I32),
-                    in_=w4_scales[:, r:16:4, :].rearrange("a q d -> q a d").bitcast(I32),
-                )
-
-        def load_ws8():
-            for r in range(4):
-                nc.sync.dma_start(out=ws[r:P:32, 0, :].bitcast(I32), in_=w8_scales[0, r:16:4, :].bitcast(I32))
-
-        def load_w8(c, n):
-            cols = slice(c * D // n, (c + 1) * D // n)
-            nc.sync.dma_start(out=w8[:, cols].bitcast(I32), in_=w8_words[0].rearrange("p d t -> p (d t)").bitcast(I32)[:, cols])
+            nc.sync.dma_start(out=raw[g][:, :, c0:c1], in_=rows[:, :, c0:c1])
 
         nc.vector.memset(ws[:].rearrange("p g d -> p (g d)").bitcast(I32), 0)
         nc.vector.memset(warm[:], 0.0)
         nc.scalar.copy(warm[:, 4:5], warm[:, 0:1])
 
-        load_dy(1, 0)
-        load_dy(1, 1)
-        load_w4(0)
-        load_ws4()
-        load_w4(1)
-        load_dy(2, 0)
-        load_dy(2, 1)
-        load_dy(0, 0)
-        load_dy(0, 1)
-        load_ws8()
-        load_w8(0, 2)
-        load_w8(1, 2)
+        load_dy(1, 0, T)
+        nc.sync.dma_start(out=w4[:].bitcast(I32), in_=w4_words.rearrange("a p b -> p a b").bitcast(I32))
+        for r in range(4):
+            nc.sync.dma_start(
+                out=ws[r:P:32, 1:3, :].bitcast(I32),
+                in_=w4_scales[:, r:16:4, :].rearrange("a q d -> q a d").bitcast(I32),
+            )
+        load_dy(2, 0, T)
+        load_dy(0, 0, T)
+        for r in range(4):
+            nc.sync.dma_start(out=ws[r:P:32, 0, :].bitcast(I32), in_=w8_scales[0, r:16:4, :].bitcast(I32))
+        w8_hbm = w8_words[0].rearrange("p d t -> p (d t)").bitcast(I32)
+        for c in range(2):
+            cols = slice(c * 512, (c + 1) * 512)
+            nc.sync.dma_start(out=w8[:, cols].bitcast(I32), in_=w8_hbm[:, cols])
 
-        def interleave(g, i):
-            dst = grouped[g][i]
-            src = raw[g][i][:].rearrange("p j t -> p t j")
-            n = dst.shape[1]
-            v = V_SHARE[n]
-            nc.vector.tensor_copy(out=dst[:, 0:v, :], in_=src[:, 0:v, :])
-            nc.scalar.copy(dst[:, v:n, :], src[:, v:n, :])
+        def interleave(g, h):
+            def views(a, b):
+                dst = grouped[g][h][:, a:b, :].rearrange("p (c i) j -> p c j i", i=4)
+                src = raw[g][:, :, h * HALF + a : h * HALF + b].rearrange("p j (c i) -> p c j i", i=4)
+                return dst, src
 
-        def quantize(g, i):
-            a, b = spans[g][i]
+            dst, src = views(0, V_COLS)
+            nc.vector.tensor_copy(out=dst, in_=src)
+            dst, src = views(V_COLS, HALF)
+            nc.scalar.copy(dst, src)
+
+        def quantize(g, h):
+            cols = slice(h * HALF, (h + 1) * HALF)
             nc.vector.quantize_mx(
-                out=codes[g][:, a:b].bitcast(E5M2X4),
-                scales=scales[g][:, a:b],
-                in_=grouped[g][i][:].rearrange("p t j -> p (t j)"),
+                out=codes[g][:, cols].bitcast(E5M2X4),
+                scales=scales[g][:, cols],
+                in_=grouped[g][h][:].rearrange("p t j -> p (t j)"),
             )
 
         def multiply(g, m, start, stop):
@@ -120,17 +104,26 @@ def tile_mix_dyq_fm_none_kernel(tc, dy, w8_words, w8_scales, w4_words, w4_scales
                 stop=stop,
             )
 
-        for g in (1, 2, 0):
-            for i in range(len(spans[g])):
-                interleave(g, i)
-                quantize(g, i)
-            if g != 0:
-                for m in range(D_TILES):
-                    multiply(g, m, g == 1, False)
-        for m in range(D_TILES):
+        def finish(m):
             multiply(0, m, False, True)
             if m % 2 == 0:
                 nc.vector.tensor_copy(out=res[m][:], in_=acc[m][:])
             else:
                 nc.scalar.copy(res[m][:], acc[m][:])
             nc.sync.dma_start(out=out[m * P : (m + 1) * P, :], in_=res[m][:])
+
+        for g in (1, 2, 0):
+            interleave(g, 0)
+            interleave(g, 1)
+            quantize(g, 0)
+            quantize(g, 1)
+            if g == 1:
+                for m in range(D_TILES):
+                    multiply(1, m, True, False)
+            if g == 2:
+                for m in range(6):
+                    multiply(2, m, False, False)
+        for m in range(D_TILES):
+            if m >= 6:
+                multiply(2, m, False, False)
+            finish(m)

@@ -16,7 +16,7 @@ PACK = 4
 K, D, T = 1536, 1024, 512
 D_TILES = D // P
 HALF = T // 2
-V_COLS = 168
+V_COLS = 144
 
 FLOPS = 2 * K * D * T
 BYTES = K * T * 4 + 512 * D + 1024 * D // 2 + 48 * D + D * T * 4
@@ -53,21 +53,29 @@ def tile_mix_dyq_fm_none_kernel(tc, dy, w8_words, w8_scales, w4_words, w4_scales
         nc.vector.memset(warm[:], 0.0)
         nc.scalar.copy(warm[:, 4:5], warm[:, 0:1])
 
-        load_dy(1, 0, T)
-        nc.sync.dma_start(out=w4[:].bitcast(I32), in_=w4_words.rearrange("a p b -> p a b").bitcast(I32))
         for r in range(4):
-            nc.sync.dma_start(
+            nc.gpsimd.dma_start(
                 out=ws[r:P:32, 1:3, :].bitcast(I32),
                 in_=w4_scales[:, r:16:4, :].rearrange("a q d -> q a d").bitcast(I32),
             )
+        for r in range(4):
+            nc.gpsimd.dma_start(out=ws[r:P:32, 0, :].bitcast(I32), in_=w8_scales[0, r:16:4, :].bitcast(I32))
+
+        def load_w4(h):
+            cols = slice(h * D, (h + 1) * D)
+            nc.sync.dma_start(out=w4[:, :, cols].bitcast(I32), in_=w4_words.rearrange("a p b -> p a b")[:, :, cols].bitcast(I32))
+
+        def load_w8(h):
+            cols = slice(h * D // 2, (h + 1) * D // 2)
+            nc.sync.dma_start(out=w8[:, cols].bitcast(I32), in_=w8_words[0].rearrange("p d t -> p (d t)").bitcast(I32)[:, cols])
+
+        load_dy(1, 0, T)
+        load_w4(0)
         load_dy(2, 0, T)
         load_dy(0, 0, T)
-        for r in range(4):
-            nc.sync.dma_start(out=ws[r:P:32, 0, :].bitcast(I32), in_=w8_scales[0, r:16:4, :].bitcast(I32))
-        w8_hbm = w8_words[0].rearrange("p d t -> p (d t)").bitcast(I32)
-        for c in range(2):
-            cols = slice(c * 512, (c + 1) * 512)
-            nc.sync.dma_start(out=w8[:, cols].bitcast(I32), in_=w8_hbm[:, cols])
+        load_w8(0)
+        load_w4(1)
+        load_w8(1)
 
         def interleave(g, h):
             def views(a, b):
@@ -117,13 +125,11 @@ def tile_mix_dyq_fm_none_kernel(tc, dy, w8_words, w8_scales, w4_words, w4_scales
             interleave(g, 1)
             quantize(g, 0)
             quantize(g, 1)
-            if g == 1:
-                for m in range(D_TILES):
-                    multiply(1, m, True, False)
-            if g == 2:
-                for m in range(6):
-                    multiply(2, m, False, False)
+            if g != 0:
+                for m in range(4):
+                    multiply(g, m, g == 1, False)
         for m in range(D_TILES):
-            if m >= 6:
+            if m >= 4:
+                multiply(1, m, True, False)
                 multiply(2, m, False, False)
             finish(m)

@@ -16,7 +16,7 @@ PACK = 4
 K, D, T = 1536, 1024, 512
 D_TILES = D // P
 HALF = T // 2
-V_COLS = 144
+V_COLS = 96
 
 FLOPS = 2 * K * D * T
 BYTES = K * T * 4 + 512 * D + 1024 * D // 2 + 48 * D + D * T * 4
@@ -35,7 +35,7 @@ def tile_mix_dyq_fm_none_kernel(tc, dy, w8_words, w8_scales, w4_words, w4_scales
         scales = []
         for g in range(3):
             raw.append(keep.tile([P, PACK, T], F32, name="raw%d" % g, align_bytes=64))
-            grouped.append([keep.tile([P, HALF, PACK], BF16, name="grouped%d%d" % (g, h), align_bytes=64) for h in range(2)])
+            grouped.append(keep.tile([P, T, PACK], BF16, name="grouped%d" % g, align_bytes=64))
             codes.append(keep.tile([P, T], U32, name="codes%d" % g, align_bytes=64))
             scales.append(keep.tile([P, T], U8, name="scales%d" % g, align_bytes=64))
         w8 = keep.tile([P, D], U32, name="w8", align_bytes=64)
@@ -53,39 +53,48 @@ def tile_mix_dyq_fm_none_kernel(tc, dy, w8_words, w8_scales, w4_words, w4_scales
         nc.vector.memset(warm[:], 0.0)
         nc.scalar.copy(warm[:, 4:5], warm[:, 0:1])
 
-        for r in range(4):
-            nc.gpsimd.dma_start(
-                out=ws[r:P:32, 1:3, :].bitcast(I32),
-                in_=w4_scales[:, r:16:4, :].rearrange("a q d -> q a d").bitcast(I32),
-            )
-        for r in range(4):
-            nc.gpsimd.dma_start(out=ws[r:P:32, 0, :].bitcast(I32), in_=w8_scales[0, r:16:4, :].bitcast(I32))
+        def load_ws4():
+            for r in range(4):
+                nc.sync.dma_start(
+                    out=ws[r:P:32, 1:3, :].bitcast(I32),
+                    in_=w4_scales[:, r:16:4, :].rearrange("a q d -> q a d").bitcast(I32),
+                )
 
-        def load_w4(h):
-            cols = slice(h * D, (h + 1) * D)
+        def load_ws8():
+            for r in range(4):
+                nc.sync.dma_start(out=ws[r:P:32, 0, :].bitcast(I32), in_=w8_scales[0, r:16:4, :].bitcast(I32))
+
+        def load_w4(a, b):
+            cols = slice(2 * a, 2 * b)
             nc.sync.dma_start(out=w4[:, :, cols].bitcast(I32), in_=w4_words.rearrange("a p b -> p a b")[:, :, cols].bitcast(I32))
 
-        def load_w8(h):
-            cols = slice(h * D // 2, (h + 1) * D // 2)
-            nc.sync.dma_start(out=w8[:, cols].bitcast(I32), in_=w8_words[0].rearrange("p d t -> p (d t)").bitcast(I32)[:, cols])
+        def load_w4p(g):
+            nc.sync.dma_start(out=w4[:, g - 1, :].bitcast(I32), in_=w4_words[g - 1].bitcast(I32))
+
+        def load_w8(a, b):
+            nc.sync.dma_start(out=w8[:, a:b].bitcast(I32), in_=w8_words[0].rearrange("p d t -> p (d t)").bitcast(I32)[:, a:b])
 
         load_dy(1, 0, T)
-        load_w4(0)
+        load_w4p(1)
+        load_ws4()
         load_dy(2, 0, T)
         load_dy(0, 0, T)
-        load_w8(0)
-        load_w4(1)
-        load_w8(1)
+        load_w4p(2)
+        load_ws8()
+        load_w8(0, 512)
+        load_w8(512, D)
 
-        def interleave(g, h):
+        def interleave(g):
             def views(a, b):
-                dst = grouped[g][h][:, a:b, :].rearrange("p (c i) j -> p c j i", i=4)
-                src = raw[g][:, :, h * HALF + a : h * HALF + b].rearrange("p j (c i) -> p c j i", i=4)
+                dst = grouped[g][:, a:b, :].rearrange("p (c i) j -> p c j i", i=4)
+                src = raw[g][:, :, a:b].rearrange("p j (c i) -> p c j i", i=4)
                 return dst, src
 
-            dst, src = views(0, V_COLS)
+            dst, src = views(0, HALF)
             nc.vector.tensor_copy(out=dst, in_=src)
-            dst, src = views(V_COLS, HALF)
+            dst, src = views(HALF, HALF + V_COLS)
+            nc.vector.tensor_copy(out=dst, in_=src)
+            dst, src = views(HALF + V_COLS, T)
             nc.scalar.copy(dst, src)
 
         def quantize(g, h):
@@ -93,7 +102,7 @@ def tile_mix_dyq_fm_none_kernel(tc, dy, w8_words, w8_scales, w4_words, w4_scales
             nc.vector.quantize_mx(
                 out=codes[g][:, cols].bitcast(E5M2X4),
                 scales=scales[g][:, cols],
-                in_=grouped[g][h][:].rearrange("p t j -> p (t j)"),
+                in_=grouped[g][:, cols, :].rearrange("p t j -> p (t j)"),
             )
 
         def multiply(g, m, start, stop):
@@ -121,15 +130,19 @@ def tile_mix_dyq_fm_none_kernel(tc, dy, w8_words, w8_scales, w4_words, w4_scales
             nc.sync.dma_start(out=out[m * P : (m + 1) * P, :], in_=res[m][:])
 
         for g in (1, 2, 0):
-            interleave(g, 0)
-            interleave(g, 1)
+            interleave(g)
             quantize(g, 0)
             quantize(g, 1)
-            if g != 0:
-                for m in range(4):
-                    multiply(g, m, g == 1, False)
+            if g == 1:
+                for m in range(D_TILES - 1):
+                    multiply(1, m, True, False)
+                for i in range(4):
+                    multiply(1, D_TILES - 1, True, True)
+                multiply(1, D_TILES - 1, True, False)
+            if g == 2:
+                for m in range(3):
+                    multiply(2, m, False, False)
         for m in range(D_TILES):
-            if m >= 4:
-                multiply(1, m, True, False)
+            if m >= 3:
                 multiply(2, m, False, False)
             finish(m)

from contextlib import ExitStack

import concourse.mybir as mybir

F32 = mybir.dt.float32
BF16 = mybir.dt.bfloat16
I32 = mybir.dt.int32
U32 = mybir.dt.uint32
U8 = mybir.dt.uint8
E4M3X4 = mybir.dt.float8_e4m3fn_x4
E5M2X4 = mybir.dt.float8_e5m2_x4
E2M1X4 = mybir.dt.float4_e2m1fn_x4

P = 128
PACK = 4
K, D, T = 1536, 1024, 512
D_TILES = D // P
HALF = T // 2
V_COLS = 96

FLOPS = 2 * K * D * T
BYTES = K * T * 4 + 512 * D + 1024 * D // 2 + 48 * D + D * T * 4


def tile_mix_dyq_fm_none_kernel(tc, dy, w8_words, w8_scales, w4_words, w4_scales, out):
    nc = tc.nc
    with ExitStack() as ctx:
        keep = ctx.enter_context(tc.tile_pool(name="keep", bufs=1))
        psum = ctx.enter_context(tc.psum_pool(name="psum", bufs=1))
        ctx.enter_context(tc.manual_schedule())

        raw = []
        grouped = []
        codes = []
        scales = []
        for g in range(3):
            raw.append(keep.tile([P, PACK, T], F32, name="raw%d" % g, align_bytes=64))
            grouped.append(keep.tile([P, T, PACK], BF16, name="grouped%d" % g, align_bytes=64))
            codes.append(keep.tile([P, T], U32, name="codes%d" % g, align_bytes=64))
            scales.append(keep.tile([P, T], U8, name="scales%d" % g, align_bytes=64))
        w8 = keep.tile([P, D], U32, name="w8", align_bytes=64)
        w4 = keep.tile([P, 2, 2 * D], U8, name="w4", align_bytes=64)
        ws = keep.tile([P, 3, D], U8, name="ws", align_bytes=64)
        warm = keep.tile([P, 8], F32, name="warm", align_bytes=64)
        acc = [psum.tile([P, T], F32, name="acc%d" % m) for m in range(D_TILES)]
        res = [keep.tile([P, T], F32, name="res%d" % m, align_bytes=64) for m in range(D_TILES)]

        def load_dy(g, c0, c1):
            rows = dy[512 * g : 512 * (g + 1), :].rearrange("(p j) t -> p j t", j=PACK)
            nc.sync.dma_start(out=raw[g][:, :, c0:c1], in_=rows[:, :, c0:c1])

        nc.vector.memset(ws[:].rearrange("p g d -> p (g d)").bitcast(I32), 0)
        nc.vector.memset(warm[:], 0.0)
        nc.scalar.copy(warm[:, 4:5], warm[:, 0:1])

        def load_ws4():
            for r in range(4):
                nc.sync.dma_start(
                    out=ws[r:P:32, 1:3, :].bitcast(I32),
                    in_=w4_scales[:, r:16:4, :].rearrange("a q d -> q a d").bitcast(I32),
                )

        def load_ws8():
            for r in range(4):
                nc.sync.dma_start(out=ws[r:P:32, 0, :].bitcast(I32), in_=w8_scales[0, r:16:4, :].bitcast(I32))

        def load_w4(a, b):
            cols = slice(2 * a, 2 * b)
            nc.sync.dma_start(out=w4[:, :, cols].bitcast(I32), in_=w4_words.rearrange("a p b -> p a b")[:, :, cols].bitcast(I32))

        def load_w4p(g):
            nc.sync.dma_start(out=w4[:, g - 1, :].bitcast(I32), in_=w4_words[g - 1].bitcast(I32))

        def load_w8(a, b):
            nc.sync.dma_start(out=w8[:, a:b].bitcast(I32), in_=w8_words[0].rearrange("p d t -> p (d t)").bitcast(I32)[:, a:b])

        load_dy(1, 0, T)
        load_w4p(1)
        load_ws4()
        load_dy(2, 0, T)
        load_dy(0, 0, T)
        load_w4p(2)
        load_ws8()
        load_w8(0, 512)
        load_w8(512, D)

        def interleave(g):
            def views(a, b):
                dst = grouped[g][:, a:b, :].rearrange("p (c i) j -> p c j i", i=4)
                src = raw[g][:, :, a:b].rearrange("p j (c i) -> p c j i", i=4)
                return dst, src

            dst, src = views(0, HALF)
            nc.vector.tensor_copy(out=dst, in_=src)
            dst, src = views(HALF, HALF + V_COLS)
            nc.vector.tensor_copy(out=dst, in_=src)
            dst, src = views(HALF + V_COLS, T)
            nc.scalar.copy(dst, src)

        def quantize(g, h):
            cols = slice(h * HALF, (h + 1) * HALF)
            nc.vector.quantize_mx(
                out=codes[g][:, cols].bitcast(E5M2X4),
                scales=scales[g][:, cols],
                in_=grouped[g][:, cols, :].rearrange("p t j -> p (t j)"),
            )

        def multiply(g, m, start, stop):
            cols = slice(m * P, (m + 1) * P)
            if g == 0:
                lhsT = w8[:, cols].bitcast(E4M3X4)
            else:
                lhsT = w4[:, g - 1, 2 * m * P : 2 * (m + 1) * P].bitcast(E2M1X4)
            nc.tensor.matmul_mx(
                out=acc[m][:],
                lhsT=lhsT,
                lhsT_scale=ws[:, g, cols],
                rhs=codes[g][:].bitcast(E5M2X4),
                rhs_scale=scales[g][:],
                start=start,
                stop=stop,
            )

        def finish(m):
            multiply(0, m, False, True)
            if m % 2 == 0:
                nc.vector.tensor_copy(out=res[m][:], in_=acc[m][:])
            else:
                nc.scalar.copy(res[m][:], acc[m][:])
            nc.sync.dma_start(out=out[m * P : (m + 1) * P, :], in_=res[m][:])

        for g in (1, 2, 0):
            interleave(g)
            quantize(g, 0)
            quantize(g, 1)
            if g == 1:
                for m in range(D_TILES - 1):
                    multiply(1, m, True, False)
                for i in range(4):
                    multiply(1, D_TILES - 1, True, True)
                multiply(1, D_TILES - 1, True, False)
            if g == 2:
                for m in range(3):
                    multiply(2, m, False, False)
        for m in range(D_TILES):
            if m >= 3:
                multiply(2, m, False, False)
            finish(m)
